import numpy as np, ml_dtypes
CORES = [17,81,89,18,82,90]
N = 6
W, KW = 64, 7
H = KW // 2
def setup_inputs(rng):
    return {"x": rng.standard_normal((N, 128, W), dtype=np.float32).astype(ml_dtypes.bfloat16), "t": rng.standard_normal((N, 128, KW * W), dtype=np.float32).astype(ml_dtypes.bfloat16)}
def setup_inputs_big(rng):
    d = setup_inputs(rng)
    for k in ("x", "t"): d[k] = (d[k].astype(np.float32) * 1024.0).astype(d[k].dtype)
    return d
def setup_inputs_small(rng):
    d = setup_inputs(rng)
    for k in ("x", "t"): d[k] = (d[k].astype(np.float32) * (1 / 1024.0)).astype(d[k].dtype)
    return d
def reference(x, t):
    X, T = x.astype(np.float64), t.astype(np.float64)
    g = np.concatenate(list(X), axis=1)
    p = np.concatenate([g[:, -H:], g, g[:, :H]], axis=1)
    y = np.stack([sum(T[r][:, W * i:W * i + W] * p[:, W * r + i:W * r + i + W] for i in range(KW)) for r in range(N)])
    return {"y": y.astype(ml_dtypes.bfloat16 if x.dtype != np.float64 else np.float64)}

@@ -1,0 +1,195 @@
+from concourse.bass import DstId, RemoteDMATransfer
+from concourse.mybir import AluOpType
+
+W, KW = 64, 7
+H = KW // 2
+X0 = 8
+KD = 4
+
+SCRATCH = {
+    "p": ("sbuf", [128, X0 + W + X0], "bfloat16"),
+    "tb": ("sbuf", [128, KW * W], "bfloat16"),
+    "pr": ("sbuf", [128, 6 * W], "float32"),
+    "a1": ("sbuf", [128, 4 * W], "float32"),
+    "a2": ("sbuf", [128, 2 * W], "float32"),
+    "ql": ("sbuf", [128, 16], "float32"),
+    "qr": ("sbuf", [128, 16], "float32"),
+    "sl": ("sbuf", [128, 8], "float32"),
+    "sr": ("sbuf", [128, 8], "float32"),
+    "yb": ("sbuf", [128, W], "bfloat16"),
+    "hl": ("sbuf", [128, 2 * H], "bfloat16"),
+    "hr": ("sbuf", [128, 2 * H], "bfloat16"),
+    "hs3": ("dram", [128, H], "bfloat16"),
+    "rb3": ("dram", [128, H], "bfloat16"),
+    "hs6": ("dram", [128, 2 * H], "bfloat16"),
+    "rb6": ("dram", [128, 2 * H], "bfloat16"),
+}
+SEMAPHORES = ["ldh", "ldx", "ldt", "sent", "rel", "arl", "arr", "v", "st"]
+
+
+def _bits(mask):
+    return [1 << b for b in range(mask.bit_length()) if (mask >> b) & 1]
+
+
+def _join(bits):
+    m = 0
+    for b in bits:
+        m |= b
+    return m
+
+
+def _relay(src, dst, cores, topo):
+    chip = topo.chip(src)
+    every = [c for c in range(topo.CHIPS * topo.CORES_PER_CHIP) if topo.chip(c) == chip]
+    cand = [c for c in every if c != src and c != dst and topo.may_write(c, dst) and topo.may_write(src, c)]
+    return min(cand, key=lambda c: (c not in cores, topo.die(c) != topo.die(src), c))
+
+
+def _plan(cores, topo):
+    n = len(cores)
+    direct, legs = {}, {}
+    for r, s in enumerate(cores):
+        for d, part, buf, sem in ((cores[(r - 1) % n], 0, "hr", "arr"), (cores[(r + 1) % n], 1, "hl", "arl")):
+            if topo.may_write(s, d):
+                direct.setdefault(s, []).append((d, part, buf, sem))
+            else:
+                legs.setdefault((s, _relay(s, d, cores, topo)), []).append((d, part, buf, sem))
+    land = {}
+    dcalls = {}
+    for s, items in direct.items():
+        common = topo.mask(s, items[0][0])
+        for it in items:
+            common &= topo.mask(s, it[0])
+        eng = _bits(common)
+        dcalls[s] = []
+        for j, (d, part, buf, sem) in enumerate(items):
+            dcalls[s].append((d, part, buf, sem, _join(eng[j * KD:(j + 1) * KD])))
+            land[(d, buf)] = (0, KD, False)
+    leg1, leg2 = {}, {}
+    for (s, m), items in legs.items():
+        assert s not in leg1 and m not in leg2
+        width = H * len(items)
+        leg1[s] = (m, width, [it[1] for it in items], _bits(topo.mask(s, m))[0])
+        used = []
+        for c in dcalls.get(m, []):
+            used += _bits(c[4])
+        if not used:
+            used = _bits(topo.mask(m, items[0][0]))[:KD * len(items)]
+        per = len(used) // len(items)
+        leg2[m] = (width, [])
+        for j, (d, part, buf, sem) in enumerate(items):
+            leg2[m][1].append((d, buf, sem, _join(used[j * per:(j + 1) * per])))
+            land[(d, buf)] = (H * j, per, True)
+    return dcalls, leg1, leg2, land
+
+
+def _issue(g, T, topo, transfers):
+    if len(transfers) == 1:
+        d, out, src, sem, mask = transfers[0]
+        rid, pid, _ = topo.addr(d)
+        g.remote_dma(out, src, sem, T.sem.sent, pid, rid, mask)
+    else:
+        lst = []
+        for d, out, src, sem, mask in transfers:
+            rid, pid, _ = topo.addr(d)
+            lst.append(RemoteDMATransfer(dst_ids=[DstId(rid=rid, pnc=pid)], dma_engine_mask=mask, remote_sem=sem,
+                                         src=src, dst=out))
+        g.remote_dma_fused(lst, local_sem=T.sem.sent)
+    return sum(len(_bits(t[4])) for t in transfers)
+
+
+def rank_program(g, core, T, topo):
+    cores = list(T.cores)
+    dcalls, leg1, leg2, land = _plan(cores, topo)
+    rank = T.rank_of(core)
+    if rank is None and core not in leg2:
+        return
+    sem = T.sem
+
+    if rank is not None:
+        loads = []
+        if core in leg1:
+            _, width, parts, _ = leg1[core]
+            stage = T["hs%d" % width]
+            for j, part in enumerate(parts):
+                out = stage[:] if len(parts) == 1 else stage[:, H * j:H * j + H]
+                loads.append((out, T.x[:, (W - H) * part:(W - H) * part + H], sem.ldh))
+        loads.append((T.p[:, X0:X0 + W], T.x[:], sem.ldx))
+        loads.append((T.tb[:], T.t[:], sem.ldt))
+        for k, (out, src, s) in enumerate(loads):
+            (g.sync, g.scalar)[k % 2].dma_start(out, src).then_inc(s, 16)
+
+    sent = 0
+    if core in leg1:
+        m, width, parts, mask = leg1[core]
+        g.wait_ge(sem.ldh, 16 * len(parts))
+        sent += _issue(g, T, topo, [(m, T["rb%d" % width][:], T["hs%d" % width][:], sem.rel, mask)])
+    if core in dcalls:
+        g.wait_ge(sem.ldx, 16)
+        sent += _issue(g, T, topo, [(d, T[buf][:, 0:H], T.p[:, X0 + (W - H) * part:X0 + (W - H) * part + H], sem[sn], mask)
+                                    for d, part, buf, sn, mask in dcalls[core]])
+    if core in leg2:
+        width, items = leg2[core]
+        g.wait_ge(sem.rel, 1)
+        sent += _issue(g, T, topo, [(d, T[buf][:, 0:width], T["rb%d" % width][:], sem[sn], mask)
+                                    for d, buf, sn, mask in items])
+    g.wait_ge(sem.sent, sent)
+    if rank is None:
+        return
+
+    v = g.vector
+    done = [0]
+
+    def op(out, a, b, o):
+        v.tensor_tensor(out=out, in0=a, in1=b, op=o).then_inc(sem.v, 1)
+        done[0] += 1
+
+    def fill(ap):
+        v.memset(ap, 0.0).then_inc(sem.v, 1)
+        done[0] += 1
+
+    def fence():
+        v.wait_ge(sem.v, done[0])
+
+    mult, add = AluOpType.mult, AluOpType.add
+    fill(T.p[:, 0:X0])
+    fill(T.p[:, X0 + W:X0 + W + X0])
+    fill(T.ql[:])
+    fill(T.qr[:])
+    v.wait_ge(sem.ldx, 16)
+    v.wait_ge(sem.ldt, 16)
+    fence()
+    for i in range(KW):
+        out = T.pr[:, W * i:W * i + W] if i < 6 else T.a1[:, 3 * W:4 * W]
+        op(out, T.tb[:, W * i:W * i + W], T.p[:, X0 - H + i:X0 - H + i + W], mult)
+    fence()
+    op(T.a1[:, 0:3 * W], T.pr[:, 0:3 * W], T.pr[:, 3 * W:6 * W], add)
+    fence()
+    op(T.a2[:], T.a1[:, 0:2 * W], T.a1[:, 2 * W:4 * W], add)
+    fence()
+    op(T.yb[:, H:W - H], T.a2[:, H:W - H], T.a2[:, W + H:2 * W - H], add)
+    op(T.ql[:, 12:12 + H], T.a2[:, 0:H], T.a2[:, W:W + H], add)
+    op(T.qr[:, 12:12 + H], T.a2[:, W - H:W], T.a2[:, 2 * W - H:2 * W], add)
+
+    sides = sorted(("hl", "hr"), key=lambda b: land[(core, b)][2])
+    for buf in sides:
+        off, count, _ = land[(core, buf)]
+        if buf == "hl":
+            v.wait_ge(sem.arl, count)
+            for i in range(H):
+                op(T.ql[:, 4 * i:4 * i + H - i], T.tb[:, W * i:W * i + H - i], T.hl[:, off + i:off + H], mult)
+            q, s, y0 = T.ql, T.sl, 0
+        else:
+            v.wait_ge(sem.arr, count)
+            for k in range(H):
+                i = KW - 1 - k
+                op(T.qr[:, 4 * k + k:4 * k + H], T.tb[:, W * i + W - H + k:W * i + W], T.hr[:, off:off + H - k], mult)
+            q, s, y0 = T.qr, T.sr, W - H
+        fence()
+        op(s[:], q[:, 0:8], q[:, 8:16], add)
+        fence()
+        op(T.yb[:, y0:y0 + H], s[:, 0:H], s[:, 4:4 + H], add)
+
+    g.sync.wait_ge(sem.v, done[0])
+    g.sync.dma_start(T.y[:], T.yb[:]).then_inc(sem.st, 16)
+    g.sync.wait_ge(sem.st, 16)

@@ -12,10 +12,11 @@ SCRATCH = {
     "pr": ("sbuf", [128, 6 * W], "float32"),
     "a1": ("sbuf", [128, 4 * W], "float32"),
     "a2": ("sbuf", [128, 2 * W], "float32"),
-    "ql": ("sbuf", [128, 16], "float32"),
-    "qr": ("sbuf", [128, 16], "float32"),
-    "sl": ("sbuf", [128, 8], "float32"),
-    "sr": ("sbuf", [128, 8], "float32"),
+    "ol": ("sbuf", [128, 4], "float32"),
+    "orr": ("sbuf", [128, 4], "float32"),
+    "tc": ("sbuf", [128, 4], "float32"),
+    "ql": ("sbuf", [128, 8], "float32"),
+    "qr": ("sbuf", [128, 8], "float32"),
     "yb": ("sbuf", [128, W], "bfloat16"),
     "hl": ("sbuf", [128, 2 * H], "bfloat16"),
     "hr": ("sbuf", [128, 2 * H], "bfloat16"),
@@ -139,56 +140,70 @@ def rank_program(g, core, T, topo):
 
     v = g.vector
     done = [0]
+    mult, add = AluOpType.mult, AluOpType.add
+
+    def count(ins):
+        ins.then_inc(sem.v, 1)
+        done[0] += 1
 
     def op(out, a, b, o):
-        v.tensor_tensor(out=out, in0=a, in1=b, op=o).then_inc(sem.v, 1)
-        done[0] += 1
+        count(v.tensor_tensor(out=out, in0=a, in1=b, op=o))
 
-    def fill(ap):
-        v.memset(ap, 0.0).then_inc(sem.v, 1)
-        done[0] += 1
+    def fma(out, a, col, plus):
+        count(v.tensor_scalar(out, a, col, plus, mult, add))
+
+    def add3(out, a, b, c):
+        count(v.tensor_tensor_scan(out, b, c, a, add, add))
 
     def fence():
         v.wait_ge(sem.v, done[0])
 
-    mult, add = AluOpType.mult, AluOpType.add
-    fill(T.p[:, 0:X0])
-    fill(T.p[:, X0 + W:X0 + W + X0])
-    fill(T.ql[:])
-    fill(T.qr[:])
+    def col(t, j):
+        return t[:, j:j + 1]
+
+    count(v.memset(T.p[:, 0:X0], 0.0))
+    count(v.memset(T.p[:, X0 + W:X0 + W + X0], 0.0))
     v.wait_ge(sem.ldx, 16)
     v.wait_ge(sem.ldt, 16)
     fence()
     for i in range(KW):
         out = T.pr[:, W * i:W * i + W] if i < 6 else T.a1[:, 3 * W:4 * W]
         op(out, T.tb[:, W * i:W * i + W], T.p[:, X0 - H + i:X0 - H + i + W], mult)
+    count(v.tensor_copy(col(T.tc, 0), col(T.tb, 2 * W)))
+    count(v.tensor_copy(col(T.tc, 1), col(T.tb, 4 * W + W - 1)))
     fence()
     op(T.a1[:, 0:3 * W], T.pr[:, 0:3 * W], T.pr[:, 3 * W:6 * W], add)
     fence()
     op(T.a2[:], T.a1[:, 0:2 * W], T.a1[:, 2 * W:4 * W], add)
     fence()
     op(T.yb[:, H:W - H], T.a2[:, H:W - H], T.a2[:, W + H:2 * W - H], add)
-    op(T.ql[:, 12:12 + H], T.a2[:, 0:H], T.a2[:, W:W + H], add)
-    op(T.qr[:, 12:12 + H], T.a2[:, W - H:W], T.a2[:, 2 * W - H:2 * W], add)
+    op(T.ol[:, 0:H], T.a2[:, 0:H], T.a2[:, W:W + H], add)
+    op(T.orr[:, 0:H], T.a2[:, W - H:W], T.a2[:, 2 * W - H:2 * W], add)
+    fence()
 
     sides = sorted(("hl", "hr"), key=lambda b: land[(core, b)][2])
     for buf in sides:
-        off, count, _ = land[(core, buf)]
+        off, count_in, _ = land[(core, buf)]
         if buf == "hl":
-            v.wait_ge(sem.arl, count)
-            for i in range(H):
-                op(T.ql[:, 4 * i:4 * i + H - i], T.tb[:, W * i:W * i + H - i], T.hl[:, off + i:off + H], mult)
-            q, s, y0 = T.ql, T.sl, 0
+            v.wait_ge(sem.arl, count_in)
+            q, o, h = T.ql, T.ol, T.hl
+            op(q[:, 0:3], T.tb[:, 0:3], h[:, off:off + 3], mult)
+            op(q[:, 4:6], T.tb[:, W:W + 2], h[:, off + 1:off + 3], mult)
+            fma(col(q, 7), col(h, off + 2), col(T.tc, 0), col(o, 0))
+            fence()
+            add3(col(T.yb, 0), col(q, 7), col(q, 0), col(q, 4))
+            add3(col(T.yb, 1), col(o, 1), col(q, 1), col(q, 5))
+            op(col(T.yb, 2), col(q, 2), col(o, 2), add)
         else:
-            v.wait_ge(sem.arr, count)
-            for k in range(H):
-                i = KW - 1 - k
-                op(T.qr[:, 4 * k + k:4 * k + H], T.tb[:, W * i + W - H + k:W * i + W], T.hr[:, off:off + H - k], mult)
-            q, s, y0 = T.qr, T.sr, W - H
-        fence()
-        op(s[:], q[:, 0:8], q[:, 8:16], add)
-        fence()
-        op(T.yb[:, y0:y0 + H], s[:, 0:H], s[:, 4:4 + H], add)
+            v.wait_ge(sem.arr, count_in)
+            q, o, h = T.qr, T.orr, T.hr
+            op(q[:, 0:3], T.tb[:, 6 * W + W - 3:6 * W + W], h[:, off:off + 3], mult)
+            op(q[:, 5:7], T.tb[:, 5 * W + W - 2:5 * W + W], h[:, off:off + 2], mult)
+            fma(col(q, 7), col(h, off), col(T.tc, 1), col(o, 2))
+            fence()
+            add3(col(T.yb, W - 1), col(q, 7), col(q, 2), col(q, 6))
+            add3(col(T.yb, W - 2), col(o, 1), col(q, 1), col(q, 5))
+            op(col(T.yb, W - 3), col(q, 0), col(o, 0), add)
 
     g.sync.wait_ge(sem.v, done[0])
     g.sync.dma_start(T.y[:], T.yb[:]).then_inc(sem.st, 16)

from concourse.bass import DstId, RemoteDMATransfer
from concourse.mybir import AluOpType

W, KW = 64, 7
H = KW // 2
X0 = 8
KD = 4

SCRATCH = {
    "p": ("sbuf", [128, X0 + W + X0], "bfloat16"),
    "tb": ("sbuf", [128, KW * W], "bfloat16"),
    "pr": ("sbuf", [128, 6 * W], "float32"),
    "a1": ("sbuf", [128, 4 * W], "float32"),
    "a2": ("sbuf", [128, 2 * W], "float32"),
    "ol": ("sbuf", [128, 4], "float32"),
    "orr": ("sbuf", [128, 4], "float32"),
    "tc": ("sbuf", [128, 4], "float32"),
    "ql": ("sbuf", [128, 8], "float32"),
    "qr": ("sbuf", [128, 8], "float32"),
    "yb": ("sbuf", [128, W], "bfloat16"),
    "hl": ("sbuf", [128, 2 * H], "bfloat16"),
    "hr": ("sbuf", [128, 2 * H], "bfloat16"),
    "hs3": ("dram", [128, H], "bfloat16"),
    "rb3": ("dram", [128, H], "bfloat16"),
    "hs6": ("dram", [128, 2 * H], "bfloat16"),
    "rb6": ("dram", [128, 2 * H], "bfloat16"),
}
SEMAPHORES = ["ldh", "ldx", "ldt", "sent", "rel", "arl", "arr", "v", "st"]


def _bits(mask):
    return [1 << b for b in range(mask.bit_length()) if (mask >> b) & 1]


def _join(bits):
    m = 0
    for b in bits:
        m |= b
    return m


def _relay(src, dst, cores, topo):
    chip = topo.chip(src)
    every = [c for c in range(topo.CHIPS * topo.CORES_PER_CHIP) if topo.chip(c) == chip]
    cand = [c for c in every if c != src and c != dst and topo.may_write(c, dst) and topo.may_write(src, c)]
    return min(cand, key=lambda c: (c not in cores, topo.die(c) != topo.die(src), c))


def _plan(cores, topo):
    n = len(cores)
    direct, legs = {}, {}
    for r, s in enumerate(cores):
        for d, part, buf, sem in ((cores[(r - 1) % n], 0, "hr", "arr"), (cores[(r + 1) % n], 1, "hl", "arl")):
            if topo.may_write(s, d):
                direct.setdefault(s, []).append((d, part, buf, sem))
            else:
                legs.setdefault((s, _relay(s, d, cores, topo)), []).append((d, part, buf, sem))
    land = {}
    dcalls = {}
    for s, items in direct.items():
        common = topo.mask(s, items[0][0])
        for it in items:
            common &= topo.mask(s, it[0])
        eng = _bits(common)
        dcalls[s] = []
        for j, (d, part, buf, sem) in enumerate(items):
            dcalls[s].append((d, part, buf, sem, _join(eng[j * KD:(j + 1) * KD])))
            land[(d, buf)] = (0, KD, False)
    leg1, leg2 = {}, {}
    for (s, m), items in legs.items():
        assert s not in leg1 and m not in leg2
        width = H * len(items)
        leg1[s] = (m, width, [it[1] for it in items], _bits(topo.mask(s, m))[0])
        used = []
        for c in dcalls.get(m, []):
            used += _bits(c[4])
        if not used:
            used = _bits(topo.mask(m, items[0][0]))[:KD * len(items)]
        per = len(used) // len(items)
        leg2[m] = (width, [])
        for j, (d, part, buf, sem) in enumerate(items):
            leg2[m][1].append((d, buf, sem, _join(used[j * per:(j + 1) * per])))
            land[(d, buf)] = (H * j, per, True)
    return dcalls, leg1, leg2, land


def _issue(g, T, topo, transfers):
    if len(transfers) == 1:
        d, out, src, sem, mask = transfers[0]
        rid, pid, _ = topo.addr(d)
        g.remote_dma(out, src, sem, T.sem.sent, pid, rid, mask)
    else:
        lst = []
        for d, out, src, sem, mask in transfers:
            rid, pid, _ = topo.addr(d)
            lst.append(RemoteDMATransfer(dst_ids=[DstId(rid=rid, pnc=pid)], dma_engine_mask=mask, remote_sem=sem,
                                         src=src, dst=out))
        g.remote_dma_fused(lst, local_sem=T.sem.sent)
    return sum(len(_bits(t[4])) for t in transfers)


def rank_program(g, core, T, topo):
    cores = list(T.cores)
    dcalls, leg1, leg2, land = _plan(cores, topo)
    rank = T.rank_of(core)
    if rank is None and core not in leg2:
        return
    sem = T.sem

    if rank is not None:
        loads = []
        if core in leg1:
            _, width, parts, _ = leg1[core]
            stage = T["hs%d" % width]
            for j, part in enumerate(parts):
                out = stage[:] if len(parts) == 1 else stage[:, H * j:H * j + H]
                loads.append((out, T.x[:, (W - H) * part:(W - H) * part + H], sem.ldh))
        loads.append((T.p[:, X0:X0 + W], T.x[:], sem.ldx))
        loads.append((T.tb[:], T.t[:], sem.ldt))
        for k, (out, src, s) in enumerate(loads):
            (g.sync, g.scalar)[k % 2].dma_start(out, src).then_inc(s, 16)

    sent = 0
    if core in leg1:
        m, width, parts, mask = leg1[core]
        g.wait_ge(sem.ldh, 16 * len(parts))
        sent += _issue(g, T, topo, [(m, T["rb%d" % width][:], T["hs%d" % width][:], sem.rel, mask)])
    if core in dcalls:
        g.wait_ge(sem.ldx, 16)
        sent += _issue(g, T, topo, [(d, T[buf][:, 0:H], T.p[:, X0 + (W - H) * part:X0 + (W - H) * part + H], sem[sn], mask)
                                    for d, part, buf, sn, mask in dcalls[core]])
    if core in leg2:
        width, items = leg2[core]
        g.wait_ge(sem.rel, 1)
        sent += _issue(g, T, topo, [(d, T[buf][:, 0:width], T["rb%d" % width][:], sem[sn], mask)
                                    for d, buf, sn, mask in items])
    g.wait_ge(sem.sent, sent)
    if rank is None:
        return

    v = g.vector
    done = [0]
    mult, add = AluOpType.mult, AluOpType.add

    def count(ins):
        ins.then_inc(sem.v, 1)
        done[0] += 1

    def op(out, a, b, o):
        count(v.tensor_tensor(out=out, in0=a, in1=b, op=o))

    def fma(out, a, col, plus):
        count(v.tensor_scalar(out, a, col, plus, mult, add))

    def add3(out, a, b, c):
        count(v.tensor_tensor_scan(out, b, c, a, add, add))

    def fence():
        v.wait_ge(sem.v, done[0])

    def col(t, j):
        return t[:, j:j + 1]

    count(v.memset(T.p[:, 0:X0], 0.0))
    count(v.memset(T.p[:, X0 + W:X0 + W + X0], 0.0))
    v.wait_ge(sem.ldx, 16)
    v.wait_ge(sem.ldt, 16)
    fence()
    for i in range(KW):
        out = T.pr[:, W * i:W * i + W] if i < 6 else T.a1[:, 3 * W:4 * W]
        op(out, T.tb[:, W * i:W * i + W], T.p[:, X0 - H + i:X0 - H + i + W], mult)
    count(v.tensor_copy(col(T.tc, 0), col(T.tb, 2 * W)))
    count(v.tensor_copy(col(T.tc, 1), col(T.tb, 4 * W + W - 1)))
    fence()
    op(T.a1[:, 0:3 * W], T.pr[:, 0:3 * W], T.pr[:, 3 * W:6 * W], add)
    fence()
    op(T.a2[:], T.a1[:, 0:2 * W], T.a1[:, 2 * W:4 * W], add)
    fence()
    op(T.yb[:, H:W - H], T.a2[:, H:W - H], T.a2[:, W + H:2 * W - H], add)
    op(T.ol[:, 0:H], T.a2[:, 0:H], T.a2[:, W:W + H], add)
    op(T.orr[:, 0:H], T.a2[:, W - H:W], T.a2[:, 2 * W - H:2 * W], add)
    fence()

    sides = sorted(("hl", "hr"), key=lambda b: land[(core, b)][2])
    for buf in sides:
        off, count_in, _ = land[(core, buf)]
        if buf == "hl":
            v.wait_ge(sem.arl, count_in)
            q, o, h = T.ql, T.ol, T.hl
            op(q[:, 0:3], T.tb[:, 0:3], h[:, off:off + 3], mult)
            op(q[:, 4:6], T.tb[:, W:W + 2], h[:, off + 1:off + 3], mult)
            fma(col(q, 7), col(h, off + 2), col(T.tc, 0), col(o, 0))
            fence()
            add3(col(T.yb, 0), col(q, 7), col(q, 0), col(q, 4))
            add3(col(T.yb, 1), col(o, 1), col(q, 1), col(q, 5))
            op(col(T.yb, 2), col(q, 2), col(o, 2), add)
        else:
            v.wait_ge(sem.arr, count_in)
            q, o, h = T.qr, T.orr, T.hr
            op(q[:, 0:3], T.tb[:, 6 * W + W - 3:6 * W + W], h[:, off:off + 3], mult)
            op(q[:, 5:7], T.tb[:, 5 * W + W - 2:5 * W + W], h[:, off:off + 2], mult)
            fma(col(q, 7), col(h, off), col(T.tc, 1), col(o, 2))
            fence()
            add3(col(T.yb, W - 1), col(q, 7), col(q, 2), col(q, 6))
            add3(col(T.yb, W - 2), col(o, 1), col(q, 1), col(q, 5))
            op(col(T.yb, W - 3), col(q, 0), col(o, 0), add)

    g.sync.wait_ge(sem.v, done[0])
    g.sync.dma_start(T.y[:], T.yb[:]).then_inc(sem.st, 16)
    g.sync.wait_ge(sem.st, 16)
